import numpy as np
import ml_dtypes


def mxq(x, axis, fmt="e4m3"):
    dtype, down = {"e4m3": (ml_dtypes.float8_e4m3fn, 7), "e5m2": (ml_dtypes.float8_e5m2, 14)}[fmt]
    v = np.moveaxis(np.asarray(x, np.float32).astype(ml_dtypes.bfloat16).astype(np.float64), axis, -1)
    blocks = v.reshape(v.shape[:-1] + (-1, 32))
    amax = np.abs(blocks).max(-1, keepdims=True)
    byte = np.maximum(np.where(amax > 0, np.frexp(amax)[1] - 1 + 127, 0) - down, 1)
    scale = np.exp2(byte - 127.0)
    codes = (blocks / scale).astype(np.float32).astype(dtype).astype(np.float64)
    return np.moveaxis((codes * scale).reshape(v.shape), -1, axis)


WIDE = False


def mx_kscale(k):
    if not WIDE:
        return np.ones(k)
    levels = np.array([30, -30])
    if k % 512:
        return np.exp2(np.random.permutation(np.resize(levels, k // 32))).repeat(32)
    a = np.empty((k // 512, 16))
    for p in range(k // 512):
        a[p, :8] = np.random.permutation(np.resize(levels, 8))
        for g in range(8):
            far = levels[np.abs(levels - a[p, g]) >= 10]
            a[p, g + 8] = far[np.random.randint(len(far))]
    return np.exp2(a.ravel()).repeat(32)


def f64(x):
    return np.asarray(x).astype(np.float64)


def striped(idx):
    return np.tile(idx.reshape(-1, 16).T, (8, 1)).astype(np.uint16)


def unstriped(offs):
    return offs[:16].T.reshape(-1).astype(np.int64)


E2M1 = np.array([0.0, 0.5, 1.0, 1.5, 2.0, 3.0, 4.0, 6.0, -0.0, -0.5, -1.0, -1.5, -2.0, -3.0, -4.0, -6.0])


def pack_weight(w, fmt):
    k, n = w.shape
    w = f64(np.asarray(w, np.float32).astype(ml_dtypes.bfloat16)).reshape(k // 32, 32, n)
    amax = np.abs(w).max(1)
    if fmt == "e4m3":
        byte = np.frexp(amax)[1] - 1 + 127 - 7
    elif fmt == "e5m2":
        byte = np.frexp(amax)[1] - 1 + 127 - 14
    else:
        mant, ex = np.frexp(amax / 6.0)
        byte = np.where(mant > 0.5, ex, ex - 1) + 127
    byte = np.clip(np.where(amax > 0, byte, 1), 1, 254)
    scaled = (w * np.exp2(127.0 - byte)[:, None, :]).reshape(k, n).astype(np.float32)
    by_word = np.ascontiguousarray(scaled.reshape(k // 512, 128, 4, n).transpose(0, 1, 3, 2))
    if fmt == "e4m3":
        words = by_word.astype(ml_dtypes.float8_e4m3fn).view(np.uint8)
    elif fmt == "e5m2":
        words = by_word.astype(ml_dtypes.float8_e5m2).view(np.uint8)
    else:
        c = by_word.astype(ml_dtypes.float4_e2m1fn).view(np.uint8) & 0xF
        words = (c[..., 0::2] | (c[..., 1::2] << 4)).reshape(k // 512, 128, 2 * n)
    return np.ascontiguousarray(words), np.ascontiguousarray(byte.astype(np.uint8).reshape(k // 512, 16, n))


def unpack_weight(words, scales, fmt):
    g, _, n = scales.shape
    words = np.ascontiguousarray(words).reshape(g, 128, n, -1)
    if fmt == "e4m3":
        vals = words.view(ml_dtypes.float8_e4m3fn).astype(np.float64)
    elif fmt == "e5m2":
        vals = words.view(ml_dtypes.float8_e5m2).astype(np.float64)
    else:
        nib = np.empty((g, 128, n, 4), np.uint8)
        nib[..., 0::2] = words & 0xF
        nib[..., 1::2] = words >> 4
        vals = E2M1[nib]
    vals = vals * np.repeat(np.exp2(scales.astype(np.float64) - 127.0), 8, axis=1)[..., None]
    return vals.transpose(0, 1, 3, 2).reshape(g * 512, n)


def d_relu2(v):
    return 2.0 * np.maximum(v, 0.0)


K, T, E, C, H, N = 256, 1024, 4, 512, 512, 512


def by_expert(wq, xq):
    return np.concatenate([wq[e].T @ xq[:, e * C:(e + 1) * C] for e in range(E)], axis=1)


def setup_inputs():
    n = np.random.standard_normal
    v = mx_kscale(N)
    u = mx_kscale(H)
    first = np.random.permutation(np.repeat(np.arange(E), T // E))
    second = (first + 1 + np.random.permutation(np.repeat(np.arange(E - 1), -(-T // (E - 1)))[:T])) % E
    while np.bincount(second, minlength=E).max() != T // E:
        load = np.bincount(second, minlength=E); hi, lo = int(load.argmax()), int(load.argmin())
        t = np.flatnonzero((second == hi) & (first != lo))[0]; second[t] = lo
    slot_token = np.empty(E * C, np.int64); pos = np.empty((2, T), np.int64); fill = np.zeros(E, np.int64)
    place = np.stack([np.random.permutation(C) for _ in range(E)])
    for r, deal in enumerate((first, second)):
        for t in np.random.permutation(T):
            e = deal[t]; j = e * C + place[e, fill[e]]; fill[e] += 1; slot_token[j] = t; pos[r, t] = j
    g = np.random.uniform(0.2, 0.8, T)
    dy = pack_weight(n((N, T)) * v[:, None], "e5m2")
    w2t = [pack_weight(m, "e2m1") for m in n((E, N, H)) / np.sqrt(N) / v[None, :, None] * u]
    w1t = pack_weight(n((H, K)) / np.sqrt(H) / u[:, None], "e4m3")
    return {
        "dy_words": dy[0],
        "dy_scales": dy[1],
        "w2t_words": np.stack([m[0] for m in w2t]),
        "w2t_scales": np.stack([m[1] for m in w2t]),
        "w1t_words": w1t[0],
        "w1t_scales": w1t[1],
        "a": (n((H, T))).astype(np.float32),
        "gate": np.stack([np.tile(g, (128, 1)), np.tile(1.0 - g, (128, 1))]).astype(np.float32),
        "offs": striped(slot_token),
        "pos1": striped(pos[0]),
        "pos2": striped(pos[1]),
    }


def reference(dy_words, dy_scales, w2t_words, w2t_scales, w1t_words, w1t_scales, a, gate, offs, pos1, pos2):
    w2t = np.stack([unpack_weight(w2t_words[e], w2t_scales[e], "e2m1") for e in range(E)])
    w1t = unpack_weight(w1t_words, w1t_scales, "e4m3")
    idx = unstriped(offs)
    gq = unpack_weight(dy_words, dy_scales, "e5m2")[:, idx]
    y = by_expert(w2t, gq)
    dh = sum(f64(gate[r, :1]) * y[:, unstriped(p)] for r, p in enumerate((pos1, pos2)))
    return w1t.T @ mxq(dh * d_relu2(f64(a)), 0, "e5m2")

@@ -1,0 +1,241 @@
+from contextlib import ExitStack
+
+import concourse.mybir as mybir
+from concourse.masks import make_identity
+
+K, T, E, C, H, N = 256, 1024, 4, 512, 512, 512
+FLOPS = 2 * N * H * E * C + 2 * H * K * T
+
+F32 = mybir.dt.float32
+BF16 = mybir.dt.bfloat16
+I32 = mybir.dt.int32
+U32 = mybir.dt.uint32
+U16 = mybir.dt.uint16
+U8 = mybir.dt.uint8
+E4X4 = mybir.dt.float8_e4m3fn_x4
+E5X4 = mybir.dt.float8_e5m2_x4
+E2X4 = mybir.dt.float4_e2m1fn_x4
+MULT = mybir.AluOpType.mult
+ADD = mybir.AluOpType.add
+COPY = mybir.ActivationFunctionType.Copy
+RELU = mybir.ActivationFunctionType.Relu
+
+P = 128
+BLOCKS = H // P
+HALF = 512
+GROUPS = [(0, 256), (256, 256), (512, 256), (768, 128), (896, 128)]
+SCALAR_TILES = (0, 1, 2, 3)
+RELU_ON_VECTOR = (0, 1)
+A_CHUNK = 256
+
+
+def tile_moe_sub_relu2_kernel(
+    tc, dy_words, dy_scales, w2t_words, w2t_scales, w1t_words, w1t_scales, a, gate, offs, pos1, pos2, out
+):
+    nc = tc.nc
+    with ExitStack() as ctx:
+        keep = ctx.enter_context(tc.tile_pool(name="keep", bufs=1))
+        ring = ctx.enter_context(tc.tile_pool(name="ring", bufs=2))
+        psum = ctx.enter_context(tc.psum_pool(name="psum", bufs=8))
+
+        offs_sb = keep.tile([P, E * C // 16], U16, name="offs_sb")
+        pos_sb = [keep.tile([P, T // 16], U16, name="pos%d_sb" % r) for r in range(2)]
+        dy_w = keep.tile([P, T], I32, name="dy_w", align_bytes=64)
+        dy_s = keep.tile([P, T], U8, name="dy_s", align_bytes=64)
+        w2_w = keep.tile([P, E, 2 * H], U8, name="w2_w", align_bytes=64)
+        w2_s = keep.tile([P, E, H], U8, name="w2_s", align_bytes=64)
+        w1_s = keep.tile([P, K], U8, name="w1_s", align_bytes=64)
+        gate_rows = keep.tile([P, P], F32, name="gate_rows")
+        gate_cols = keep.tile([P, 16], F32, name="gate_cols")
+        ident = keep.tile([P, P], F32, name="ident")
+        r_sb = [keep.tile([P, BLOCKS, A_CHUNK], F32, name="r_sb%d" % c) for c in range(T // A_CHUNK)]
+        slot_w = [keep.tile([P, C], U32, name="slot_w%d" % e, tag="slot_w%d" % (e % 2), align_bytes=64) for e in range(E)]
+        slot_s = [keep.tile([P, C], U8, name="slot_s%d" % e, tag="slot_s%d" % e, align_bytes=64) for e in range(E)]
+        a_sb = [
+            keep.tile([P, BLOCKS, A_CHUNK], F32, name="a_sb%d" % c, tag=tenant, align_bytes=64)
+            for c, tenant in enumerate(("slot_s0", "slot_s1", "slot_s2", "slot_s3"))
+        ]
+        w1_w = keep.tile([P, K], I32, name="w1_w", tag="slot_w0", align_bytes=64)
+        y = [keep.tile([P, E * C], F32, name="y%d" % b) for b in range(BLOCKS)]
+        da_w = [keep.tile([P, HALF], U32, name="da_w%d" % h, align_bytes=64) for h in range(T // HALF)]
+        da_s = [keep.tile([P, HALF], U8, name="da_s%d" % h, align_bytes=64) for h in range(T // HALF)]
+
+        nc.gpsimd.memset(dy_s[:].bitcast(I32), 0)
+        nc.vector.memset(w2_s[:].rearrange("p e c -> p (e c)").bitcast(I32), 0)
+        nc.vector.memset(w1_s[:].bitcast(I32), 0)
+        nc.vector.memset(gate_rows[:], 0.0)
+        make_identity(nc, ident[:])
+
+        def load_dy_words():
+            nc.sync.dma_start(dy_w[:], dy_words[0].rearrange("p t d -> p (t d)").bitcast(I32))
+
+        def load_dy_scales():
+            rows = dy_scales[0].rearrange("(q r) t -> r q t", r=4)
+            for r in range(4):
+                nc.sync.dma_start(dy_s[r:P:32, :].bitcast(I32), rows[r].bitcast(I32))
+
+        def load_w2_words():
+            nc.sync.dma_start(w2_w[:].bitcast(I32), w2t_words[:, 0].rearrange("e p c -> p e c").bitcast(I32))
+
+        def load_w2_scales():
+            rows = w2t_scales[:, 0].rearrange("e (q r) c -> r q e c", r=4)
+            for r in range(4):
+                nc.sync.dma_start(w2_s[r:P:32, :, :].bitcast(I32), rows[r].bitcast(I32))
+
+        def load_a(c):
+            nc.sync.dma_start(
+                a_sb[c][:], a[:, c * A_CHUNK : (c + 1) * A_CHUNK].rearrange("(b p) t -> p b t", p=P)
+            )
+
+        nc.sync.dma_start(offs_sb[:], offs)
+        load_dy_words()
+        load_dy_scales()
+        load_w2_words()
+        load_w2_scales()
+        nc.sync.dma_start(pos_sb[0][:], pos1)
+        nc.sync.dma_start(pos_sb[1][:], pos2)
+        for r in range(2):
+            nc.sync.dma_start(gate_rows[8 * r : 8 * r + 8, :], gate[r, 0].rearrange("(j c) -> j c", c=P))
+        w1_rows = w1t_scales[0].rearrange("(q r) k -> r q k", r=4)
+        for r in range(4):
+            nc.sync.dma_start(w1_s[r:P:32, :].bitcast(I32), w1_rows[r].bitcast(I32))
+
+        def gather_expert(e):
+            slots = offs_sb[:, e * (C // 16) : (e + 1) * (C // 16)]
+            nc.vector.tensor_copy(slot_w[e][:], dy_w[:].bitcast(U32).indirect(slots))
+            nc.vector.tensor_copy(slot_s[e][:], dy_s[:].indirect(slots))
+
+        def expert_block(e, b):
+            acc = psum.tile([P, C], F32, name="bank")
+            nc.tensor.matmul_mx(
+                out=acc[:],
+                lhsT=w2_w[:, e, 2 * P * b : 2 * P * (b + 1)].bitcast(E2X4),
+                lhsT_scale=w2_s[:, e, P * b : P * (b + 1)],
+                rhs=slot_w[e][:].bitcast(E5X4),
+                rhs_scale=slot_s[e][:],
+                start=True,
+                stop=True,
+            )
+            nc.scalar.copy(y[b][:, e * C : (e + 1) * C], acc[:])
+
+        for e in range(2):
+            gather_expert(e)
+            for b in range(BLOCKS):
+                expert_block(e, b)
+        gather_expert(2)
+        gather_expert(3)
+        for b in range(BLOCKS):
+            expert_block(2, b)
+            expert_block(3, b)
+
+        for c in range(0, T // A_CHUNK):
+            load_a(c)
+        nc.sync.dma_start(w1_w[:], w1t_words[0].rearrange("p k d -> p (k d)").bitcast(I32))
+
+        gate_ps = psum.tile([P, C], F32, name="bank")
+        nc.tensor.transpose(gate_ps[:, 0:P], gate_rows[:], ident[:])
+        nc.scalar.activation(gate_cols[:], gate_ps[:, 0:16], COPY, scale=2.0)
+
+        def relu(c):
+            if c in RELU_ON_VECTOR:
+                nc.vector.tensor_scalar_max(r_sb[c][:], a_sb[c][:], 0.0)
+            else:
+                nc.scalar.activation(r_sb[c][:], a_sb[c][:], RELU)
+
+        def gather(t0, n, order):
+            got = {}
+            c, c0 = divmod(t0, A_CHUNK)
+            for b, r in order:
+                prod = ring.tile([P, n], F32, name="prod", tag="prod%d%d%d" % (b, r, t0), bufs=1)
+                nc.vector.tensor_tensor(
+                    prod[:],
+                    y[b][:].indirect(pos_sb[r][:, t0 // 16 : (t0 + n) // 16]),
+                    r_sb[c][:, b, c0 : c0 + n],
+                    MULT,
+                )
+                got[b, r] = prod
+            return got
+
+        def combine(got, t0, n):
+            grouped = ring.tile([P, n, 4], BF16, name="grouped", align_bytes=64, bufs=3)
+            for u in range(n // P):
+                j = t0 // P + u
+                turned = []
+                for r in range(2):
+                    bank = psum.tile([P, H], F32, name="bank")
+                    for b in range(BLOCKS):
+                        nc.tensor.transpose(bank[:, P * b : P * (b + 1)], got[b, r][:, P * u : P * (u + 1)], ident[:])
+                    turned.append(bank)
+                g1 = gate_cols[:, j : j + 1]
+                g2 = gate_cols[:, 8 + j : 9 + j]
+                dst = grouped[:, P * u : P * (u + 1), :]
+                back = psum.tile([P, 4, P], F32, name="bank")
+                if j in SCALAR_TILES:
+                    parts = []
+                    for bank, g in ((turned[0], g1), (turned[1], g2)):
+                        part = ring.tile([P, 4, P], F32, name="part", bufs=4)
+                        nc.scalar.activation(part[:], bank[:].rearrange("t (p d) -> t d p", d=4), COPY, scale=g)
+                        parts.append(part)
+                    for d in range(4):
+                        for r in range(2):
+                            nc.tensor.matmul(
+                                back[:, d, :], parts[r][:, d, :], ident[:], start=(r == 0), stop=(r == 1), is_transpose=True
+                            )
+                    nc.scalar.copy(dst, back[:].rearrange("p d t -> p t d"))
+                else:
+                    part = ring.tile([P, H], F32, name="part", bufs=4)
+                    nc.scalar.activation(part[:], turned[0][:], COPY, scale=g1)
+                    da_t = ring.tile([P, H], BF16, name="da_t", bufs=3)
+                    nc.vector.scalar_tensor_tensor(da_t[:], turned[1][:], g2, part[:], MULT, ADD)
+                    words = da_t[:].bitcast(F32)
+                    for w in range(2):
+                        nc.tensor.transpose(back[:, w, :], words[:, w : H // 2 : 2], ident[:])
+                    nc.scalar.copy(dst.bitcast(F32), back[:, 0:2, :].rearrange("p w t -> p t w"))
+            return grouped
+
+        def quantize(grouped, t0, n):
+            h, c0 = divmod(t0, HALF)
+            nc.vector.quantize_mx(
+                out=da_w[h][:, c0 : c0 + n].bitcast(E5X4),
+                scales=da_s[h][:, c0 : c0 + n],
+                in_=grouped[:].rearrange("p t d -> p (t d)"),
+            )
+
+        def project(h):
+            for kb in range(K // P):
+                acc = psum.tile([P, HALF], F32, name="bank")
+                nc.tensor.matmul_mx(
+                    out=acc[:],
+                    lhsT=w1_w[:, P * kb : P * (kb + 1)].bitcast(E4X4),
+                    lhsT_scale=w1_s[:, P * kb : P * (kb + 1)],
+                    rhs=da_w[h][:].bitcast(E5X4),
+                    rhs_scale=da_s[h][:],
+                    start=True,
+                    stop=True,
+                )
+                res = ring.tile([P, HALF], F32, name="res", bufs=4)
+                if h == T // HALF - 1 and kb == 1:
+                    nc.vector.tensor_copy(res[:], acc[:])
+                else:
+                    nc.scalar.copy(res[:], acc[:])
+                nc.sync.dma_start(out[P * kb : P * (kb + 1), HALF * h : HALF * (h + 1)], res[:])
+
+        by_block = [(b, r) for b in range(BLOCKS) for r in range(2)]
+        by_list = [(b, r) for r in range(2) for b in range(BLOCKS)]
+        for c in RELU_ON_VECTOR:
+            relu(c)
+        relu_done = set(RELU_ON_VECTOR)
+        waiting = None
+        for idx, (t0, n) in enumerate(GROUPS):
+            got = gather(t0, n, by_block if idx == 0 else by_list)
+            nxt = (t0 + n) // A_CHUNK
+            if nxt < T // A_CHUNK and nxt not in relu_done:
+                relu(nxt)
+                relu_done.add(nxt)
+            if waiting is not None:
+                quantize(*waiting)
+                if (waiting[1] + waiting[2]) % HALF == 0:
+                    project(waiting[1] // HALF)
+            waiting = (combine(got, t0, n), t0, n)
+        quantize(*waiting)
+        project(T // HALF - 1)

@@ -1,7 +1,6 @@
 from contextlib import ExitStack
 
 import concourse.mybir as mybir
-from concourse.masks import make_identity
 
 K, T, E, C, H, N = 256, 1024, 4, 512, 512, 512
 FLOPS = 2 * N * H * E * C + 2 * H * K * T
@@ -17,16 +16,13 @@ E5X4 = mybir.dt.float8_e5m2_x4
 E2X4 = mybir.dt.float4_e2m1fn_x4
 MULT = mybir.AluOpType.mult
 ADD = mybir.AluOpType.add
+MAX = mybir.AluOpType.max
 COPY = mybir.ActivationFunctionType.Copy
-RELU = mybir.ActivationFunctionType.Relu
 
 P = 128
-BLOCKS = H // P
+PACK = 4
 HALF = 512
-GROUPS = [(0, 256), (256, 256), (512, 256), (768, 128), (896, 128)]
-SCALAR_TILES = (0, 1, 2, 3)
-RELU_ON_VECTOR = (0, 1)
-A_CHUNK = 256
+GROUPS = [(0, 512, 2), (512, 256, 2), (768, 128, 4), (896, 128, 2)]
 
 
 def tile_moe_sub_relu2_kernel(
@@ -35,166 +31,120 @@ def tile_moe_sub_relu2_kernel(
     nc = tc.nc
     with ExitStack() as ctx:
         keep = ctx.enter_context(tc.tile_pool(name="keep", bufs=1))
-        ring = ctx.enter_context(tc.tile_pool(name="ring", bufs=2))
         psum = ctx.enter_context(tc.psum_pool(name="psum", bufs=8))
 
         offs_sb = keep.tile([P, E * C // 16], U16, name="offs_sb")
         pos_sb = [keep.tile([P, T // 16], U16, name="pos%d_sb" % r) for r in range(2)]
-        dy_w = keep.tile([P, T], I32, name="dy_w", align_bytes=64)
-        dy_s = keep.tile([P, T], U8, name="dy_s", align_bytes=64)
-        w2_w = keep.tile([P, E, 2 * H], U8, name="w2_w", align_bytes=64)
-        w2_s = keep.tile([P, E, H], U8, name="w2_s", align_bytes=64)
+        dy_w = keep.tile([P, T], I32, name="dy_w", tag="dy_w", align_bytes=64)
+        dy_s = keep.tile([P, T], U8, name="dy_s", tag="dy_s", align_bytes=64)
+        w2_w = keep.tile([P, E * 2 * H], U8, name="w2_w", align_bytes=64)
+        w2_s = keep.tile([P, E * H], U8, name="w2_s", align_bytes=64)
+        w1_w = keep.tile([P, K], I32, name="w1_w", align_bytes=64)
         w1_s = keep.tile([P, K], U8, name="w1_s", align_bytes=64)
-        gate_rows = keep.tile([P, P], F32, name="gate_rows")
-        gate_cols = keep.tile([P, 16], F32, name="gate_cols")
-        ident = keep.tile([P, P], F32, name="ident")
-        r_sb = [keep.tile([P, BLOCKS, A_CHUNK], F32, name="r_sb%d" % c) for c in range(T // A_CHUNK)]
-        slot_w = [keep.tile([P, C], U32, name="slot_w%d" % e, tag="slot_w%d" % (e % 2), align_bytes=64) for e in range(E)]
-        slot_s = [keep.tile([P, C], U8, name="slot_s%d" % e, tag="slot_s%d" % e, align_bytes=64) for e in range(E)]
-        a_sb = [
-            keep.tile([P, BLOCKS, A_CHUNK], F32, name="a_sb%d" % c, tag=tenant, align_bytes=64)
-            for c, tenant in enumerate(("slot_s0", "slot_s1", "slot_s2", "slot_s3"))
-        ]
-        w1_w = keep.tile([P, K], I32, name="w1_w", tag="slot_w0", align_bytes=64)
-        y = [keep.tile([P, E * C], F32, name="y%d" % b) for b in range(BLOCKS)]
+        gate_sb = [keep.tile([P, T], F32, name="gate_sb%d" % r) for r in range(2)]
+        a_sb = [keep.tile([P, PACK, HALF], F32, name="a_sb%d" % h) for h in range(T // HALF)]
+        slot_w = [keep.tile([P, C], U32, name="slot_w%d" % e, align_bytes=64) for e in range(E)]
+        slot_s = [keep.tile([P, C], U8, name="slot_s%d" % e, align_bytes=64) for e in range(E)]
+        y = [keep.tile([P, E * C], F32, name="y%d" % d) for d in range(PACK)]
         da_w = [keep.tile([P, HALF], U32, name="da_w%d" % h, align_bytes=64) for h in range(T // HALF)]
         da_s = [keep.tile([P, HALF], U8, name="da_s%d" % h, align_bytes=64) for h in range(T // HALF)]
 
-        nc.gpsimd.memset(dy_s[:].bitcast(I32), 0)
-        nc.vector.memset(w2_s[:].rearrange("p e c -> p (e c)").bitcast(I32), 0)
+        nc.vector.memset(dy_s[:].bitcast(I32), 0)
+        nc.vector.memset(w2_s[:].bitcast(I32), 0)
         nc.vector.memset(w1_s[:].bitcast(I32), 0)
-        nc.vector.memset(gate_rows[:], 0.0)
-        make_identity(nc, ident[:])
-
-        def load_dy_words():
-            nc.sync.dma_start(dy_w[:], dy_words[0].rearrange("p t d -> p (t d)").bitcast(I32))
-
-        def load_dy_scales():
-            rows = dy_scales[0].rearrange("(q r) t -> r q t", r=4)
-            for r in range(4):
-                nc.sync.dma_start(dy_s[r:P:32, :].bitcast(I32), rows[r].bitcast(I32))
-
-        def load_w2_words():
-            nc.sync.dma_start(w2_w[:].bitcast(I32), w2t_words[:, 0].rearrange("e p c -> p e c").bitcast(I32))
-
-        def load_w2_scales():
-            rows = w2t_scales[:, 0].rearrange("e (q r) c -> r q e c", r=4)
-            for r in range(4):
-                nc.sync.dma_start(w2_s[r:P:32, :, :].bitcast(I32), rows[r].bitcast(I32))
-
-        def load_a(c):
-            nc.sync.dma_start(
-                a_sb[c][:], a[:, c * A_CHUNK : (c + 1) * A_CHUNK].rearrange("(b p) t -> p b t", p=P)
-            )
 
         nc.sync.dma_start(offs_sb[:], offs)
-        load_dy_words()
-        load_dy_scales()
-        load_w2_words()
-        load_w2_scales()
+        dy_rows = dy_scales[0].rearrange("(q r) t -> r q t", r=4)
+        for r in range(4):
+            queue = nc.scalar if r % 2 else nc.sync
+            queue.dma_start(dy_s[r:P:32, :].bitcast(I32), dy_rows[r].bitcast(I32))
+        nc.sync.dma_start(
+            w2_w[:].rearrange("p (e c) -> p e c", e=E).bitcast(I32),
+            w2t_words[:, 0].rearrange("e p c -> p e c").bitcast(I32),
+        )
+        nc.sync.dma_start(dy_w[:], dy_words[0].rearrange("p t d -> p (t d)").bitcast(I32))
+        w2_rows = w2t_scales[:, 0].rearrange("e (q r) c -> r q e c", r=4)
+        w1_rows = w1t_scales[0].rearrange("(q r) k -> r q k", r=4)
+        for r in range(4):
+            nc.scalar.dma_start(
+                w2_s[r:P:32, :].rearrange("p (e c) -> p e c", e=E).bitcast(I32), w2_rows[r].bitcast(I32)
+            )
         nc.sync.dma_start(pos_sb[0][:], pos1)
         nc.sync.dma_start(pos_sb[1][:], pos2)
         for r in range(2):
-            nc.sync.dma_start(gate_rows[8 * r : 8 * r + 8, :], gate[r, 0].rearrange("(j c) -> j c", c=P))
-        w1_rows = w1t_scales[0].rearrange("(q r) k -> r q k", r=4)
+            nc.sync.dma_start(gate_sb[r][:], gate[r])
+        a_rows = a.rearrange("(p d) t -> p d t", d=PACK)
+        for h in range(T // HALF):
+            nc.sync.dma_start(a_sb[h][:], a_rows[:, :, HALF * h : HALF * (h + 1)])
+        nc.sync.dma_start(w1_w[:], w1t_words[0].rearrange("p k d -> p (k d)").bitcast(I32))
         for r in range(4):
             nc.sync.dma_start(w1_s[r:P:32, :].bitcast(I32), w1_rows[r].bitcast(I32))
+
+        def regroup(d0, tags):
+            words = keep.tile([P, 2, 2 * E * P], U8, name="plane_w%d" % d0, tag=tags[0], align_bytes=64)
+            scales = keep.tile([P, 2, E * P], U8, name="plane_s%d" % d0, tag=tags[1], align_bytes=64)
+            nc.vector.tensor_copy(
+                words[:].bitcast(U16),
+                w2_w[:].bitcast(U16).rearrange("p (m d) -> p d m", d=PACK)[:, d0 : d0 + 2, :],
+            )
+            nc.vector.tensor_copy(scales[:], w2_s[:].rearrange("p (m d) -> p d m", d=PACK)[:, d0 : d0 + 2, :])
+            return words, scales
 
         def gather_expert(e):
             slots = offs_sb[:, e * (C // 16) : (e + 1) * (C // 16)]
             nc.vector.tensor_copy(slot_w[e][:], dy_w[:].bitcast(U32).indirect(slots))
             nc.vector.tensor_copy(slot_s[e][:], dy_s[:].indirect(slots))
 
-        def expert_block(e, b):
+        def expert_plane(e, d, planes):
+            words, scales = planes
             acc = psum.tile([P, C], F32, name="bank")
             nc.tensor.matmul_mx(
                 out=acc[:],
-                lhsT=w2_w[:, e, 2 * P * b : 2 * P * (b + 1)].bitcast(E2X4),
-                lhsT_scale=w2_s[:, e, P * b : P * (b + 1)],
+                lhsT=words[:, d % 2, 2 * P * e : 2 * P * (e + 1)].bitcast(E2X4),
+                lhsT_scale=scales[:, d % 2, P * e : P * (e + 1)],
                 rhs=slot_w[e][:].bitcast(E5X4),
                 rhs_scale=slot_s[e][:],
                 start=True,
                 stop=True,
             )
-            nc.scalar.copy(y[b][:, e * C : (e + 1) * C], acc[:])
+            nc.scalar.activation(y[d][:, e * C : (e + 1) * C], acc[:], COPY, scale=2.0)
 
-        for e in range(2):
+        first = regroup(0, ("plane_w", "plane_s"))
+        for e in range(E):
             gather_expert(e)
-            for b in range(BLOCKS):
-                expert_block(e, b)
-        gather_expert(2)
-        gather_expert(3)
-        for b in range(BLOCKS):
-            expert_block(2, b)
-            expert_block(3, b)
+            for d in range(2):
+                expert_plane(e, d, first)
+        second = regroup(2, ("dy_w", "late_s"))
+        for d in range(2, PACK):
+            for e in range(E):
+                expert_plane(e, d, second)
 
-        for c in range(0, T // A_CHUNK):
-            load_a(c)
-        nc.sync.dma_start(w1_w[:], w1t_words[0].rearrange("p k d -> p (k d)").bitcast(I32))
-
-        gate_ps = psum.tile([P, C], F32, name="bank")
-        nc.tensor.transpose(gate_ps[:, 0:P], gate_rows[:], ident[:])
-        nc.scalar.activation(gate_cols[:], gate_ps[:, 0:16], COPY, scale=2.0)
-
-        def relu(c):
-            if c in RELU_ON_VECTOR:
-                nc.vector.tensor_scalar_max(r_sb[c][:], a_sb[c][:], 0.0)
-            else:
-                nc.scalar.activation(r_sb[c][:], a_sb[c][:], RELU)
-
-        def gather(t0, n, order):
-            got = {}
-            c, c0 = divmod(t0, A_CHUNK)
-            for b, r in order:
-                prod = ring.tile([P, n], F32, name="prod", tag="prod%d%d%d" % (b, r, t0), bufs=1)
-                nc.vector.tensor_tensor(
-                    prod[:],
-                    y[b][:].indirect(pos_sb[r][:, t0 // 16 : (t0 + n) // 16]),
-                    r_sb[c][:, b, c0 : c0 + n],
-                    MULT,
-                )
-                got[b, r] = prod
-            return got
-
-        def combine(got, t0, n):
-            grouped = ring.tile([P, n, 4], BF16, name="grouped", align_bytes=64, bufs=3)
-            for u in range(n // P):
-                j = t0 // P + u
-                turned = []
-                for r in range(2):
-                    bank = psum.tile([P, H], F32, name="bank")
-                    for b in range(BLOCKS):
-                        nc.tensor.transpose(bank[:, P * b : P * (b + 1)], got[b, r][:, P * u : P * (u + 1)], ident[:])
-                    turned.append(bank)
-                g1 = gate_cols[:, j : j + 1]
-                g2 = gate_cols[:, 8 + j : 9 + j]
-                dst = grouped[:, P * u : P * (u + 1), :]
-                back = psum.tile([P, 4, P], F32, name="bank")
-                if j in SCALAR_TILES:
-                    parts = []
-                    for bank, g in ((turned[0], g1), (turned[1], g2)):
-                        part = ring.tile([P, 4, P], F32, name="part", bufs=4)
-                        nc.scalar.activation(part[:], bank[:].rearrange("t (p d) -> t d p", d=4), COPY, scale=g)
-                        parts.append(part)
-                    for d in range(4):
-                        for r in range(2):
-                            nc.tensor.matmul(
-                                back[:, d, :], parts[r][:, d, :], ident[:], start=(r == 0), stop=(r == 1), is_transpose=True
-                            )
-                    nc.scalar.copy(dst, back[:].rearrange("p d t -> p t d"))
-                else:
-                    part = ring.tile([P, H], F32, name="part", bufs=4)
-                    nc.scalar.activation(part[:], turned[0][:], COPY, scale=g1)
-                    da_t = ring.tile([P, H], BF16, name="da_t", bufs=3)
-                    nc.vector.scalar_tensor_tensor(da_t[:], turned[1][:], g2, part[:], MULT, ADD)
-                    words = da_t[:].bitcast(F32)
-                    for w in range(2):
-                        nc.tensor.transpose(back[:, w, :], words[:, w : H // 2 : 2], ident[:])
-                    nc.scalar.copy(dst.bitcast(F32), back[:, 0:2, :].rearrange("p w t -> p t w"))
-            return grouped
-
-        def quantize(grouped, t0, n):
+        def combine(t0, n, span):
             h, c0 = divmod(t0, HALF)
+            prods = [keep.tile([P, PACK, n], F32, name="prod%d_%d" % (r, t0)) for r in range(2)]
+            total = keep.tile([P, PACK, n], F32, name="total%d" % t0)
+            da = keep.tile([P, PACK, n], BF16, name="da%d" % t0)
+            for d in range(PACK):
+                for r in range(2):
+                    nc.vector.tensor_tensor(
+                        prods[r][:, d, :],
+                        y[d][:].indirect(pos_sb[r][:, t0 // 16 : (t0 + n) // 16]),
+                        gate_sb[r][:, t0 : t0 + n],
+                        MULT,
+                    )
+                if (d + 1) % span == 0:
+                    ds = slice(d + 1 - span, d + 1)
+                    nc.vector.tensor_tensor(total[:, ds, :], prods[0][:, ds, :], prods[1][:, ds, :], ADD)
+                    nc.vector.scalar_tensor_tensor(
+                        da[:, ds, :], a_sb[h][:, ds, c0 : c0 + n], 0.0, total[:, ds, :], MAX, MULT
+                    )
+            grouped = keep.tile([P, n, PACK], BF16, name="grouped%d" % t0, align_bytes=64)
+            dst = grouped[:].rearrange("p (c i) d -> p c d i", i=4)
+            src = da[:].rearrange("p d (c i) -> p c d i", i=4)
+            if t0 + n == T:
+                nc.vector.tensor_copy(dst, src)
+            else:
+                nc.scalar.copy(dst, src)
             nc.vector.quantize_mx(
                 out=da_w[h][:, c0 : c0 + n].bitcast(E5X4),
                 scales=da_s[h][:, c0 : c0 + n],
@@ -213,29 +163,14 @@ def tile_moe_sub_relu2_kernel(
                     start=True,
                     stop=True,
                 )
-                res = ring.tile([P, HALF], F32, name="res", bufs=4)
+                res = keep.tile([P, HALF], F32, name="res%d%d" % (h, kb))
                 if h == T // HALF - 1 and kb == 1:
                     nc.vector.tensor_copy(res[:], acc[:])
                 else:
                     nc.scalar.copy(res[:], acc[:])
                 nc.sync.dma_start(out[P * kb : P * (kb + 1), HALF * h : HALF * (h + 1)], res[:])
 
-        by_block = [(b, r) for b in range(BLOCKS) for r in range(2)]
-        by_list = [(b, r) for r in range(2) for b in range(BLOCKS)]
-        for c in RELU_ON_VECTOR:
-            relu(c)
-        relu_done = set(RELU_ON_VECTOR)
-        waiting = None
-        for idx, (t0, n) in enumerate(GROUPS):
-            got = gather(t0, n, by_block if idx == 0 else by_list)
-            nxt = (t0 + n) // A_CHUNK
-            if nxt < T // A_CHUNK and nxt not in relu_done:
-                relu(nxt)
-                relu_done.add(nxt)
-            if waiting is not None:
-                quantize(*waiting)
-                if (waiting[1] + waiting[2]) % HALF == 0:
-                    project(waiting[1] // HALF)
-            waiting = (combine(got, t0, n), t0, n)
-        quantize(*waiting)
-        project(T // HALF - 1)
+        for t0, n, span in GROUPS:
+            combine(t0, n, span)
+            if (t0 + n) % HALF == 0:
+                project(t0 // HALF)

@@ -1,6 +1,7 @@
 from contextlib import ExitStack
 
 import concourse.mybir as mybir
+from concourse.masks import make_identity
 
 K, T, E, C, H, N = 256, 1024, 4, 512, 512, 512
 FLOPS = 2 * N * H * E * C + 2 * H * K * T
@@ -18,11 +19,12 @@ MULT = mybir.AluOpType.mult
 ADD = mybir.AluOpType.add
 MAX = mybir.AluOpType.max
 COPY = mybir.ActivationFunctionType.Copy
+RELU = mybir.ActivationFunctionType.Relu
 
 P = 128
 PACK = 4
 HALF = 512
-GROUPS = [(0, 512, 2), (512, 256, 2), (768, 128, 4), (896, 128, 2)]
+TURNED = 384
 
 
 def tile_moe_sub_relu2_kernel(
@@ -31,7 +33,7 @@ def tile_moe_sub_relu2_kernel(
     nc = tc.nc
     with ExitStack() as ctx:
         keep = ctx.enter_context(tc.tile_pool(name="keep", bufs=1))
-        psum = ctx.enter_context(tc.psum_pool(name="psum", bufs=8))
+        psum = ctx.enter_context(tc.psum_pool(name="psum", bufs=3))
 
         offs_sb = keep.tile([P, E * C // 16], U16, name="offs_sb")
         pos_sb = [keep.tile([P, T // 16], U16, name="pos%d_sb" % r) for r in range(2)]
@@ -41,8 +43,21 @@ def tile_moe_sub_relu2_kernel(
         w2_s = keep.tile([P, E * H], U8, name="w2_s", align_bytes=64)
         w1_w = keep.tile([P, K], I32, name="w1_w", align_bytes=64)
         w1_s = keep.tile([P, K], U8, name="w1_s", align_bytes=64)
-        gate_sb = [keep.tile([P, T], F32, name="gate_sb%d" % r) for r in range(2)]
-        a_sb = [keep.tile([P, PACK, HALF], F32, name="a_sb%d" % h) for h in range(T // HALF)]
+        gate_sb = [keep.tile([P, T - TURNED], F32, name="gate_sb%d" % r) for r in range(2)]
+        gate_rows = keep.tile([P, P], F32, name="gate_rows")
+        woven = {
+            t0: keep.tile([P, PACK * n], BF16, name="woven%d" % t0, align_bytes=64)
+            for t0, n in ((512, 256), (768, 128), (896, 128))
+        }
+        gate_cols = [woven[t0][:, 0:8].bitcast(F32) for t0 in (512, 768)]
+        ident = keep.tile([P, P], F32, name="ident")
+        mask_tile = keep.tile([P, PACK - 1, TURNED], F32, name="mask_tile")
+        twice = keep.tile([P, 2 * (T - TURNED)], F32, name="twice")
+        mid = T - TURNED - TURNED // 2
+        mask = [mask_tile[:, 0, :], mask_tile[:, 1, :], twice[:, mid : mid + TURNED], mask_tile[:, 2, :]]
+        gate2 = [twice[:, r * (T - TURNED) : (r + 1) * (T - TURNED)] for r in range(2)]
+        a_turned = keep.tile([P, PACK, TURNED], F32, name="a_turned")
+        a_plain = keep.tile([P, PACK, T - TURNED], F32, name="a_plain")
         slot_w = [keep.tile([P, C], U32, name="slot_w%d" % e, align_bytes=64) for e in range(E)]
         slot_s = [keep.tile([P, C], U8, name="slot_s%d" % e, align_bytes=64) for e in range(E)]
         y = [keep.tile([P, E * C], F32, name="y%d" % d) for d in range(PACK)]
@@ -52,6 +67,8 @@ def tile_moe_sub_relu2_kernel(
         nc.vector.memset(dy_s[:].bitcast(I32), 0)
         nc.vector.memset(w2_s[:].bitcast(I32), 0)
         nc.vector.memset(w1_s[:].bitcast(I32), 0)
+        nc.vector.memset(gate_rows[:], 0.0)
+        make_identity(nc, ident[:])
 
         nc.sync.dma_start(offs_sb[:], offs)
         dy_rows = dy_scales[0].rearrange("(q r) t -> r q t", r=4)
@@ -62,6 +79,8 @@ def tile_moe_sub_relu2_kernel(
             w2_w[:].rearrange("p (e c) -> p e c", e=E).bitcast(I32),
             w2t_words[:, 0].rearrange("e p c -> p e c").bitcast(I32),
         )
+        a_rows = a.rearrange("(p d) t -> p d t", d=PACK)
+        nc.sync.dma_start(a_turned[:], a_rows[:, :, 0:TURNED])
         nc.sync.dma_start(dy_w[:], dy_words[0].rearrange("p t d -> p (t d)").bitcast(I32))
         w2_rows = w2t_scales[:, 0].rearrange("e (q r) c -> r q e c", r=4)
         w1_rows = w1t_scales[0].rearrange("(q r) k -> r q k", r=4)
@@ -72,10 +91,10 @@ def tile_moe_sub_relu2_kernel(
         nc.sync.dma_start(pos_sb[0][:], pos1)
         nc.sync.dma_start(pos_sb[1][:], pos2)
         for r in range(2):
-            nc.sync.dma_start(gate_sb[r][:], gate[r])
-        a_rows = a.rearrange("(p d) t -> p d t", d=PACK)
-        for h in range(T // HALF):
-            nc.sync.dma_start(a_sb[h][:], a_rows[:, :, HALF * h : HALF * (h + 1)])
+            nc.sync.dma_start(gate_rows[4 * r : 4 * r + 4, :], gate[r, 0, 0:HALF].rearrange("(j c) -> j c", c=P))
+        for r in range(2):
+            nc.sync.dma_start(gate_sb[r][:], gate[r, :, TURNED:T])
+        nc.sync.dma_start(a_plain[:], a_rows[:, :, TURNED:T])
         nc.sync.dma_start(w1_w[:], w1t_words[0].rearrange("p k d -> p (k d)").bitcast(I32))
         for r in range(4):
             nc.sync.dma_start(w1_s[r:P:32, :].bitcast(I32), w1_rows[r].bitcast(I32))
@@ -107,7 +126,15 @@ def tile_moe_sub_relu2_kernel(
                 start=True,
                 stop=True,
             )
-            nc.scalar.activation(y[d][:, e * C : (e + 1) * C], acc[:], COPY, scale=2.0)
+            nc.scalar.copy(y[d][:, e * C : (e + 1) * C], acc[:])
+
+        nc.scalar.activation(mask_tile[:, 0:2, :], a_turned[:, 0:2, :], RELU)
+        for d in range(2, PACK):
+            nc.scalar.activation(mask[d], a_turned[:, d, :], RELU)
+        gate_ps = psum.tile([P, P], F32, name="turned", bufs=5)
+        nc.tensor.transpose(gate_ps[:], gate_rows[:], ident[:])
+        for r in range(2):
+            nc.scalar.activation(gate_cols[r], gate_ps[:, 4 * r : 4 * r + 4], COPY, scale=2.0)
 
         first = regroup(0, ("plane_w", "plane_s"))
         for e in range(E):
@@ -119,36 +146,84 @@ def tile_moe_sub_relu2_kernel(
             for e in range(E):
                 expert_plane(e, d, second)
 
-        def combine(t0, n, span):
+        early = keep.tile([P, HALF], F32, name="early", align_bytes=64)
+        shared = keep.tile([P, HALF], F32, name="shared", align_bytes=64)
+
+        def gather(dst, d, r, t0, n, factor):
+            nc.vector.tensor_tensor(dst, y[d][:].indirect(pos_sb[r][:, t0 // 16 : (t0 + n) // 16]), factor, MULT)
+
+        def finish(prods, da, t0, n, ds):
+            c0 = t0 - TURNED
+            total = keep.tile([P, ds.stop - ds.start, n], F32, name="total%d_%d" % (t0, ds.start))
+            nc.vector.tensor_tensor(total[:], prods[0][:, ds, :], prods[1][:, ds, :], ADD)
+            nc.vector.scalar_tensor_tensor(da[:, ds, :], a_plain[:, ds, c0 : c0 + n], 0.0, total[:], MAX, MULT)
+
+        def weave(engine_copy, dst, da):
+            engine_copy(dst.rearrange("p (c i d) -> p c d i", i=4, d=PACK), da[:].rearrange("p d (c i) -> p c d i", i=4))
+
+        def round_turned(j, back):
+            dst = (early if j < 2 else shared)[:, 2 * P * (j % 2) : 2 * P * (j % 2 + 1)].bitcast(BF16)
+            nc.scalar.copy(dst.rearrange("p (t d) -> p t d", d=PACK), back[:].rearrange("p d t -> p t d"))
+
+        def first_half():
+            tiles = TURNED // P
+            rest = HALF - TURNED
+            turned = [[psum.tile([P, H], F32, name="turned", bufs=5) for r in range(2)] for j in range(tiles)]
+            prods = [keep.tile([P, PACK, rest], F32, name="rest%d" % r) for r in range(2)]
+            da = keep.tile([P, PACK, rest], BF16, name="da_rest")
+            masked = {}
+            for d in range(PACK):
+                for r in range(2):
+                    masked[d, r] = keep.tile([P, TURNED], F32, name="masked%d%d" % (d, r))
+                    gather(masked[d, r][:], d, r, 0, TURNED, mask[d])
+                    for j in range(2):
+                        nc.tensor.transpose(
+                            turned[j][r][:, P * d : P * (d + 1)], masked[d, r][:, P * j : P * (j + 1)], ident[:]
+                        )
+            for r in range(2):
+                nc.scalar.activation(gate2[r], gate_sb[r][:], COPY, scale=2.0)
+            for j in range(tiles):
+                parts = [keep.tile([P, H], F32, name="part%d_%d" % (r, j)) for r in range(2)]
+                for r in range(2):
+                    if j >= 2:
+                        for d in range(PACK):
+                            nc.tensor.transpose(
+                                turned[j][r][:, P * d : P * (d + 1)], masked[d, r][:, P * j : P * (j + 1)], ident[:]
+                            )
+                    nc.scalar.activation(parts[r][:], turned[j][r][:], COPY, scale=gate_cols[r][:, j : j + 1])
+                back = psum.tile([P, PACK, P], F32, name="turned", bufs=5)
+                for d in range(PACK):
+                    for r in range(2):
+                        nc.tensor.matmul(
+                            back[:, d, :],
+                            parts[r][:, P * d : P * (d + 1)],
+                            ident[:],
+                            start=(r == 0),
+                            stop=(r == 1),
+                            is_transpose=True,
+                        )
+                round_turned(j, back)
+            for d in range(PACK):
+                for r in range(2):
+                    gather(prods[r][:, d, :], d, r, TURNED, rest, gate2[r][:, 0:rest])
+            finish(prods, da, TURNED, rest, slice(0, PACK))
+            weave(nc.scalar.copy, shared[:, 2 * P : 4 * P].bitcast(BF16), da)
+
+        def combine(t0, n, cuts, borrowed):
             h, c0 = divmod(t0, HALF)
-            prods = [keep.tile([P, PACK, n], F32, name="prod%d_%d" % (r, t0)) for r in range(2)]
-            total = keep.tile([P, PACK, n], F32, name="total%d" % t0)
+            if borrowed:
+                prods = [source[:].rearrange("p (d t) -> p d t", d=PACK) for source in (early, shared)]
+            else:
+                prods = [keep.tile([P, PACK, n], F32, name="prod%d_%d" % (r, t0))[:] for r in range(2)]
             da = keep.tile([P, PACK, n], BF16, name="da%d" % t0)
             for d in range(PACK):
                 for r in range(2):
-                    nc.vector.tensor_tensor(
-                        prods[r][:, d, :],
-                        y[d][:].indirect(pos_sb[r][:, t0 // 16 : (t0 + n) // 16]),
-                        gate_sb[r][:, t0 : t0 + n],
-                        MULT,
-                    )
-                if (d + 1) % span == 0:
-                    ds = slice(d + 1 - span, d + 1)
-                    nc.vector.tensor_tensor(total[:, ds, :], prods[0][:, ds, :], prods[1][:, ds, :], ADD)
-                    nc.vector.scalar_tensor_tensor(
-                        da[:, ds, :], a_sb[h][:, ds, c0 : c0 + n], 0.0, total[:, ds, :], MAX, MULT
-                    )
-            grouped = keep.tile([P, n, PACK], BF16, name="grouped%d" % t0, align_bytes=64)
-            dst = grouped[:].rearrange("p (c i) d -> p c d i", i=4)
-            src = da[:].rearrange("p d (c i) -> p c d i", i=4)
-            if t0 + n == T:
-                nc.vector.tensor_copy(dst, src)
-            else:
-                nc.scalar.copy(dst, src)
+                    gather(prods[r][:, d, :], d, r, t0, n, gate2[r][:, t0 - TURNED : t0 - TURNED + n])
+                if d + 1 in cuts:
+                    finish(prods, da, t0, n, slice(cuts[d + 1], d + 1))
+            weave(nc.vector.tensor_copy if t0 + n == T else nc.scalar.copy, woven[t0][:], da)
             nc.vector.quantize_mx(
-                out=da_w[h][:, c0 : c0 + n].bitcast(E5X4),
-                scales=da_s[h][:, c0 : c0 + n],
-                in_=grouped[:].rearrange("p t d -> p (t d)"),
+                out=da_w[h][:, c0 : c0 + n].bitcast(E5X4), scales=da_s[h][:, c0 : c0 + n], in_=woven[t0][:]
             )
 
         def project(h):
@@ -170,7 +245,16 @@ def tile_moe_sub_relu2_kernel(
                     nc.scalar.copy(res[:], acc[:])
                 nc.sync.dma_start(out[P * kb : P * (kb + 1), HALF * h : HALF * (h + 1)], res[:])
 
-        for t0, n, span in GROUPS:
-            combine(t0, n, span)
-            if (t0 + n) % HALF == 0:
-                project(t0 // HALF)
+        first_half()
+        combine(512, 256, {2: 0, 4: 2}, False)
+        combine(768, 128, {4: 0}, False)
+        for c0, source in ((0, early), (2 * P, shared)):
+            nc.vector.quantize_mx(
+                out=da_w[0][:, c0 : c0 + 2 * P].bitcast(E5X4),
+                scales=da_s[0][:, c0 : c0 + 2 * P],
+                in_=source[:].bitcast(BF16),
+            )
+        project(0)
+
+        combine(896, 128, {3: 0, 4: 3}, True)
+        project(1)

@@ -12,9 +12,9 @@ I32 = mybir.dt.int32
 U32 = mybir.dt.uint32
 U16 = mybir.dt.uint16
 U8 = mybir.dt.uint8
-E4X4 = mybir.dt.float8_e4m3fn_x4
-E5X4 = mybir.dt.float8_e5m2_x4
-E2X4 = mybir.dt.float4_e2m1fn_x4
+E4M3X4 = mybir.dt.float8_e4m3fn_x4
+E5M2X4 = mybir.dt.float8_e5m2_x4
+E2M1X4 = mybir.dt.float4_e2m1fn_x4
 MULT = mybir.AluOpType.mult
 ADD = mybir.AluOpType.add
 MAX = mybir.AluOpType.max
@@ -24,7 +24,13 @@ RELU = mybir.ActivationFunctionType.Relu
 P = 128
 PACK = 4
 HALF = 512
+LIST_ROWS = 16
 TURNED = 384
+TILES = TURNED // P
+PLAIN = T - TURNED
+MIDDLE, LATE, LAST = (TURNED, 384), (768, P), (896, P)
+MATMUL_BANKS = 3
+TURN_BANKS = 5
 
 
 def tile_moe_sub_relu2_kernel(
@@ -33,36 +39,37 @@ def tile_moe_sub_relu2_kernel(
     nc = tc.nc
     with ExitStack() as ctx:
         keep = ctx.enter_context(tc.tile_pool(name="keep", bufs=1))
-        psum = ctx.enter_context(tc.psum_pool(name="psum", bufs=3))
+        reuse = ctx.enter_context(tc.tile_pool(name="reuse", bufs=1))
+        psum = ctx.enter_context(tc.psum_pool(name="psum", bufs=MATMUL_BANKS))
 
-        offs_sb = keep.tile([P, E * C // 16], U16, name="offs_sb")
-        pos_sb = [keep.tile([P, T // 16], U16, name="pos%d_sb" % r) for r in range(2)]
-        dy_w = keep.tile([P, T], I32, name="dy_w", tag="dy_w", align_bytes=64)
-        dy_s = keep.tile([P, T], U8, name="dy_s", tag="dy_s", align_bytes=64)
+        offs_sb = keep.tile([P, E * C // LIST_ROWS], U16, name="offs_sb")
+        pos_sb = [keep.tile([P, T // LIST_ROWS], U16, name="pos%d_sb" % r) for r in range(2)]
+        dy_w = reuse.tile([P, T], I32, name="dy_w", align_bytes=64, offset=0)
+        dy_s = keep.tile([P, T], U8, name="dy_s", align_bytes=64)
         w2_w = keep.tile([P, E * 2 * H], U8, name="w2_w", align_bytes=64)
         w2_s = keep.tile([P, E * H], U8, name="w2_s", align_bytes=64)
         w1_w = keep.tile([P, K], I32, name="w1_w", align_bytes=64)
         w1_s = keep.tile([P, K], U8, name="w1_s", align_bytes=64)
-        gate_sb = [keep.tile([P, T - TURNED], F32, name="gate_sb%d" % r) for r in range(2)]
+        gate_sb = [keep.tile([P, PLAIN], F32, name="gate_sb%d" % r) for r in range(2)]
         gate_rows = keep.tile([P, P], F32, name="gate_rows")
-        woven = {
-            t0: keep.tile([P, PACK * n], BF16, name="woven%d" % t0, align_bytes=64)
-            for t0, n in ((512, 256), (768, 128), (896, 128))
-        }
-        gate_cols = [woven[t0][:, 0:8].bitcast(F32) for t0 in (512, 768)]
         ident = keep.tile([P, P], F32, name="ident")
-        mask_tile = keep.tile([P, PACK - 1, TURNED], F32, name="mask_tile")
-        twice = keep.tile([P, 2 * (T - TURNED)], F32, name="twice")
-        mid = T - TURNED - TURNED // 2
-        mask = [mask_tile[:, 0, :], mask_tile[:, 1, :], twice[:, mid : mid + TURNED], mask_tile[:, 2, :]]
-        gate2 = [twice[:, r * (T - TURNED) : (r + 1) * (T - TURNED)] for r in range(2)]
         a_turned = keep.tile([P, PACK, TURNED], F32, name="a_turned")
-        a_plain = keep.tile([P, PACK, T - TURNED], F32, name="a_plain")
+        a_plain = keep.tile([P, PACK, PLAIN], F32, name="a_plain")
         slot_w = [keep.tile([P, C], U32, name="slot_w%d" % e, align_bytes=64) for e in range(E)]
         slot_s = [keep.tile([P, C], U8, name="slot_s%d" % e, align_bytes=64) for e in range(E)]
         y = [keep.tile([P, E * C], F32, name="y%d" % d) for d in range(PACK)]
         da_w = [keep.tile([P, HALF], U32, name="da_w%d" % h, align_bytes=64) for h in range(T // HALF)]
         da_s = [keep.tile([P, HALF], U8, name="da_s%d" % h, align_bytes=64) for h in range(T // HALF)]
+
+        woven_head = keep.tile([P, 2 * LATE[0]], F32, name="woven_head", align_bytes=64)
+        woven_late = keep.tile([P, 2 * LATE[1]], F32, name="woven_late", align_bytes=64)
+        woven_last = keep.tile([P, 2 * LAST[1]], F32, name="woven_last", align_bytes=64)
+        gate_cols = [woven_head[:, 2 * HALF : 2 * HALF + TILES], woven_late[:, 0:TILES]]
+        twice = keep.tile([P, 2 * PLAIN], F32, name="twice")
+        gate2 = [twice[:, r * PLAIN : (r + 1) * PLAIN] for r in range(2)]
+        mask_tile = keep.tile([P, PACK - 1, TURNED], F32, name="mask_tile")
+        straddle = twice[:, PLAIN - TURNED // 2 : PLAIN + TURNED // 2]
+        mask = [mask_tile[:, 0, :], mask_tile[:, 1, :], straddle, mask_tile[:, 2, :]]
 
         nc.vector.memset(dy_s[:].bitcast(I32), 0)
         nc.vector.memset(w2_s[:].bitcast(I32), 0)
@@ -91,7 +98,9 @@ def tile_moe_sub_relu2_kernel(
         nc.sync.dma_start(pos_sb[0][:], pos1)
         nc.sync.dma_start(pos_sb[1][:], pos2)
         for r in range(2):
-            nc.sync.dma_start(gate_rows[4 * r : 4 * r + 4, :], gate[r, 0, 0:HALF].rearrange("(j c) -> j c", c=P))
+            nc.sync.dma_start(
+                gate_rows[TILES * r : TILES * (r + 1), :], gate[r, 0, 0:TURNED].rearrange("(j c) -> j c", c=P)
+            )
         for r in range(2):
             nc.sync.dma_start(gate_sb[r][:], gate[r, :, TURNED:T])
         nc.sync.dma_start(a_plain[:], a_rows[:, :, TURNED:T])
@@ -99,29 +108,25 @@ def tile_moe_sub_relu2_kernel(
         for r in range(4):
             nc.sync.dma_start(w1_s[r:P:32, :].bitcast(I32), w1_rows[r].bitcast(I32))
 
-        def regroup(d0, tags):
-            words = keep.tile([P, 2, 2 * E * P], U8, name="plane_w%d" % d0, tag=tags[0], align_bytes=64)
-            scales = keep.tile([P, 2, E * P], U8, name="plane_s%d" % d0, tag=tags[1], align_bytes=64)
+        def regroup(d0, words, scales):
             nc.vector.tensor_copy(
                 words[:].bitcast(U16),
                 w2_w[:].bitcast(U16).rearrange("p (m d) -> p d m", d=PACK)[:, d0 : d0 + 2, :],
             )
             nc.vector.tensor_copy(scales[:], w2_s[:].rearrange("p (m d) -> p d m", d=PACK)[:, d0 : d0 + 2, :])
-            return words, scales
 
         def gather_expert(e):
-            slots = offs_sb[:, e * (C // 16) : (e + 1) * (C // 16)]
+            slots = offs_sb[:, e * (C // LIST_ROWS) : (e + 1) * (C // LIST_ROWS)]
             nc.vector.tensor_copy(slot_w[e][:], dy_w[:].bitcast(U32).indirect(slots))
             nc.vector.tensor_copy(slot_s[e][:], dy_s[:].indirect(slots))
 
-        def expert_plane(e, d, planes):
-            words, scales = planes
+        def expert_plane(e, d, words, scales):
             acc = psum.tile([P, C], F32, name="bank")
             nc.tensor.matmul_mx(
                 out=acc[:],
-                lhsT=words[:, d % 2, 2 * P * e : 2 * P * (e + 1)].bitcast(E2X4),
+                lhsT=words[:, d % 2, 2 * P * e : 2 * P * (e + 1)].bitcast(E2M1X4),
                 lhsT_scale=scales[:, d % 2, P * e : P * (e + 1)],
-                rhs=slot_w[e][:].bitcast(E5X4),
+                rhs=slot_w[e][:].bitcast(E5M2X4),
                 rhs_scale=slot_s[e][:],
                 start=True,
                 stop=True,
@@ -131,67 +136,53 @@ def tile_moe_sub_relu2_kernel(
         nc.scalar.activation(mask_tile[:, 0:2, :], a_turned[:, 0:2, :], RELU)
         for d in range(2, PACK):
             nc.scalar.activation(mask[d], a_turned[:, d, :], RELU)
-        gate_ps = psum.tile([P, P], F32, name="turned", bufs=5)
+        gate_ps = psum.tile([P, P], F32, name="turned", bufs=TURN_BANKS)
         nc.tensor.transpose(gate_ps[:], gate_rows[:], ident[:])
         for r in range(2):
-            nc.scalar.activation(gate_cols[r], gate_ps[:, 4 * r : 4 * r + 4], COPY, scale=2.0)
+            nc.scalar.activation(gate_cols[r], gate_ps[:, TILES * r : TILES * (r + 1)], COPY, scale=2.0)
 
-        first = regroup(0, ("plane_w", "plane_s"))
+        early_w = keep.tile([P, 2, 2 * E * P], U8, name="early_w", align_bytes=64)
+        early_s = keep.tile([P, 2, E * P], U8, name="early_s", align_bytes=64)
+        regroup(0, early_w, early_s)
         for e in range(E):
             gather_expert(e)
             for d in range(2):
-                expert_plane(e, d, first)
-        second = regroup(2, ("dy_w", "late_s"))
+                expert_plane(e, d, early_w, early_s)
+        late_w = reuse.tile([P, 2, 2 * E * P], U8, name="late_w", align_bytes=64, offset=0)
+        late_s = reuse.tile([P, 2, E * P], U8, name="late_s", align_bytes=64, offset=4 * E * P)
+        regroup(2, late_w, late_s)
         for d in range(2, PACK):
             for e in range(E):
-                expert_plane(e, d, second)
-
-        early = keep.tile([P, HALF], F32, name="early", align_bytes=64)
-        shared = keep.tile([P, HALF], F32, name="shared", align_bytes=64)
+                expert_plane(e, d, late_w, late_s)
 
         def gather(dst, d, r, t0, n, factor):
-            nc.vector.tensor_tensor(dst, y[d][:].indirect(pos_sb[r][:, t0 // 16 : (t0 + n) // 16]), factor, MULT)
+            picks = pos_sb[r][:, t0 // LIST_ROWS : (t0 + n) // LIST_ROWS]
+            nc.vector.tensor_tensor(dst, y[d][:].indirect(picks), factor, MULT)
 
-        def finish(prods, da, t0, n, ds):
-            c0 = t0 - TURNED
-            total = keep.tile([P, ds.stop - ds.start, n], F32, name="total%d_%d" % (t0, ds.start))
-            nc.vector.tensor_tensor(total[:], prods[0][:, ds, :], prods[1][:, ds, :], ADD)
-            nc.vector.scalar_tensor_tensor(da[:, ds, :], a_plain[:, ds, c0 : c0 + n], 0.0, total[:], MAX, MULT)
+        def turn(bank, masked, d, j):
+            nc.tensor.transpose(bank[:, P * d : P * (d + 1)], masked[:, P * j : P * (j + 1)], ident[:])
 
-        def weave(engine_copy, dst, da):
-            engine_copy(dst.rearrange("p (c i d) -> p c d i", i=4, d=PACK), da[:].rearrange("p d (c i) -> p c d i", i=4))
-
-        def round_turned(j, back):
-            dst = (early if j < 2 else shared)[:, 2 * P * (j % 2) : 2 * P * (j % 2 + 1)].bitcast(BF16)
-            nc.scalar.copy(dst.rearrange("p (t d) -> p t d", d=PACK), back[:].rearrange("p d t -> p t d"))
-
-        def first_half():
-            tiles = TURNED // P
-            rest = HALF - TURNED
-            turned = [[psum.tile([P, H], F32, name="turned", bufs=5) for r in range(2)] for j in range(tiles)]
-            prods = [keep.tile([P, PACK, rest], F32, name="rest%d" % r) for r in range(2)]
-            da = keep.tile([P, PACK, rest], BF16, name="da_rest")
+        def turned_road():
+            turned = [
+                [psum.tile([P, H], F32, name="turned", bufs=TURN_BANKS) for r in range(2)] for j in range(TILES)
+            ]
             masked = {}
             for d in range(PACK):
                 for r in range(2):
                     masked[d, r] = keep.tile([P, TURNED], F32, name="masked%d%d" % (d, r))
                     gather(masked[d, r][:], d, r, 0, TURNED, mask[d])
-                    for j in range(2):
-                        nc.tensor.transpose(
-                            turned[j][r][:, P * d : P * (d + 1)], masked[d, r][:, P * j : P * (j + 1)], ident[:]
-                        )
+                    for j in range(TILES - 1):
+                        turn(turned[j][r], masked[d, r], d, j)
             for r in range(2):
                 nc.scalar.activation(gate2[r], gate_sb[r][:], COPY, scale=2.0)
-            for j in range(tiles):
+            for j in range(TILES):
                 parts = [keep.tile([P, H], F32, name="part%d_%d" % (r, j)) for r in range(2)]
                 for r in range(2):
-                    if j >= 2:
+                    if j == TILES - 1:
                         for d in range(PACK):
-                            nc.tensor.transpose(
-                                turned[j][r][:, P * d : P * (d + 1)], masked[d, r][:, P * j : P * (j + 1)], ident[:]
-                            )
+                            turn(turned[j][r], masked[d, r], d, j)
                     nc.scalar.activation(parts[r][:], turned[j][r][:], COPY, scale=gate_cols[r][:, j : j + 1])
-                back = psum.tile([P, PACK, P], F32, name="turned", bufs=5)
+                back = psum.tile([P, PACK, P], F32, name="turned", bufs=TURN_BANKS)
                 for d in range(PACK):
                     for r in range(2):
                         nc.tensor.matmul(
@@ -202,59 +193,64 @@ def tile_moe_sub_relu2_kernel(
                             stop=(r == 1),
                             is_transpose=True,
                         )
-                round_turned(j, back)
-            for d in range(PACK):
-                for r in range(2):
-                    gather(prods[r][:, d, :], d, r, TURNED, rest, gate2[r][:, 0:rest])
-            finish(prods, da, TURNED, rest, slice(0, PACK))
-            weave(nc.scalar.copy, shared[:, 2 * P : 4 * P].bitcast(BF16), da)
+                dst = woven_head[:, 2 * P * j : 2 * P * (j + 1)].bitcast(BF16)
+                nc.scalar.copy(dst.rearrange("p (t d) -> p t d", d=PACK), back[:].rearrange("p d t -> p t d"))
 
-        def combine(t0, n, cuts, borrowed):
-            h, c0 = divmod(t0, HALF)
-            if borrowed:
-                prods = [source[:].rearrange("p (d t) -> p d t", d=PACK) for source in (early, shared)]
-            else:
-                prods = [keep.tile([P, PACK, n], F32, name="prod%d_%d" % (r, t0))[:] for r in range(2)]
+        def plain_road(group, cuts, prods, woven, weaver):
+            t0, n = group
+            c0 = t0 - TURNED
             da = keep.tile([P, PACK, n], BF16, name="da%d" % t0)
-            for d in range(PACK):
-                for r in range(2):
-                    gather(prods[r][:, d, :], d, r, t0, n, gate2[r][:, t0 - TURNED : t0 - TURNED + n])
-                if d + 1 in cuts:
-                    finish(prods, da, t0, n, slice(cuts[d + 1], d + 1))
-            weave(nc.vector.tensor_copy if t0 + n == T else nc.scalar.copy, woven[t0][:], da)
-            nc.vector.quantize_mx(
-                out=da_w[h][:, c0 : c0 + n].bitcast(E5X4), scales=da_s[h][:, c0 : c0 + n], in_=woven[t0][:]
+            for d0, d1 in cuts:
+                for d in range(d0, d1):
+                    for r in range(2):
+                        gather(prods[r][:, d, :], d, r, t0, n, gate2[r][:, c0 : c0 + n])
+                dh = keep.tile([P, d1 - d0, n], F32, name="dh%d_%d" % (t0, d0))
+                nc.vector.tensor_tensor(dh[:], prods[0][:, d0:d1, :], prods[1][:, d0:d1, :], ADD)
+                nc.vector.scalar_tensor_tensor(da[:, d0:d1, :], a_plain[:, d0:d1, c0 : c0 + n], 0.0, dh[:], MAX, MULT)
+            weaver(
+                woven.bitcast(BF16).rearrange("p (c i d) -> p c d i", i=4, d=PACK),
+                da[:].rearrange("p d (c i) -> p c d i", i=4),
             )
 
-        def project(h):
+        def own_products(group):
+            return [keep.tile([P, PACK, group[1]], F32, name="prod%d_%d" % (r, group[0]))[:] for r in range(2)]
+
+        def quantize(t0, n, woven):
+            h, c0 = divmod(t0, HALF)
+            nc.vector.quantize_mx(
+                out=da_w[h][:, c0 : c0 + n].bitcast(E5M2X4), scales=da_s[h][:, c0 : c0 + n], in_=woven.bitcast(BF16)
+            )
+
+        def project(h, movers, pieces):
+            width = HALF // pieces
             for kb in range(K // P):
                 acc = psum.tile([P, HALF], F32, name="bank")
                 nc.tensor.matmul_mx(
                     out=acc[:],
-                    lhsT=w1_w[:, P * kb : P * (kb + 1)].bitcast(E4X4),
+                    lhsT=w1_w[:, P * kb : P * (kb + 1)].bitcast(E4M3X4),
                     lhsT_scale=w1_s[:, P * kb : P * (kb + 1)],
-                    rhs=da_w[h][:].bitcast(E5X4),
+                    rhs=da_w[h][:].bitcast(E5M2X4),
                     rhs_scale=da_s[h][:],
                     start=True,
                     stop=True,
                 )
-                res = keep.tile([P, HALF], F32, name="res%d%d" % (h, kb))
-                if h == T // HALF - 1 and kb == 1:
-                    nc.vector.tensor_copy(res[:], acc[:])
-                else:
-                    nc.scalar.copy(res[:], acc[:])
-                nc.sync.dma_start(out[P * kb : P * (kb + 1), HALF * h : HALF * (h + 1)], res[:])
+                for c0 in range(0, HALF, width):
+                    res = keep.tile([P, width], F32, name="res%d_%d_%d" % (h, kb, c0))
+                    movers[kb](res[:], acc[:, c0 : c0 + width])
+                    nc.sync.dma_start(out[P * kb : P * (kb + 1), HALF * h + c0 : HALF * h + c0 + width], res[:])
 
-        first_half()
-        combine(512, 256, {2: 0, 4: 2}, False)
-        combine(768, 128, {4: 0}, False)
-        for c0, source in ((0, early), (2 * P, shared)):
-            nc.vector.quantize_mx(
-                out=da_w[0][:, c0 : c0 + 2 * P].bitcast(E5X4),
-                scales=da_s[0][:, c0 : c0 + 2 * P],
-                in_=source[:].bitcast(BF16),
-            )
-        project(0)
-
-        combine(896, 128, {3: 0, 4: 3}, True)
-        project(1)
+        turned_road()
+        plain_road(MIDDLE, ((0, 2), (2, 4)), own_products(MIDDLE), woven_head[:, 2 * MIDDLE[0] :], nc.scalar.copy)
+        quantize(HALF, LATE[0] - HALF, woven_head[:, 2 * HALF :])
+        plain_road(LATE, ((0, 4),), own_products(LATE), woven_late[:], nc.scalar.copy)
+        quantize(LATE[0], LATE[1], woven_late[:])
+        quarter = HALF // 2
+        for t0 in (0, quarter):
+            quantize(t0, quarter, woven_head[:, 2 * t0 : 2 * (t0 + quarter)])
+        project(0, (nc.scalar.copy, nc.scalar.copy), 1)
+        borrowed = [
+            woven_head[:, HALF * r : HALF * (r + 1)].rearrange("p (d t) -> p d t", d=PACK) for r in range(2)
+        ]
+        plain_road(LAST, ((0, 3), (3, 4)), borrowed, woven_last[:], nc.vector.tensor_copy)
+        quantize(LAST[0], LAST[1], woven_last[:])
+        project(1, (nc.scalar.copy, nc.vector.tensor_copy), 2)

@@ -25,10 +25,11 @@ P = 128
 PACK = 4
 HALF = 512
 LIST_ROWS = 16
-TURNED = 384
+TURNED = 512
 TILES = TURNED // P
+LEAD = TURNED - P
 PLAIN = T - TURNED
-MIDDLE, LATE, LAST = (TURNED, 384), (768, P), (896, P)
+MIDDLE, LATE, LAST = (TURNED, 2 * P), (768, P), (896, P)
 MATMUL_BANKS = 3
 TURN_BANKS = 5
 
@@ -64,12 +65,13 @@ def tile_moe_sub_relu2_kernel(
         woven_head = keep.tile([P, 2 * LATE[0]], F32, name="woven_head", align_bytes=64)
         woven_late = keep.tile([P, 2 * LATE[1]], F32, name="woven_late", align_bytes=64)
         woven_last = keep.tile([P, 2 * LAST[1]], F32, name="woven_last", align_bytes=64)
-        gate_cols = [woven_head[:, 2 * HALF : 2 * HALF + TILES], woven_late[:, 0:TILES]]
+        gate_cols = [woven_head[:, 2 * MIDDLE[0] : 2 * MIDDLE[0] + TILES], woven_late[:, 0:TILES]]
         twice = keep.tile([P, 2 * PLAIN], F32, name="twice")
         gate2 = [twice[:, r * PLAIN : (r + 1) * PLAIN] for r in range(2)]
-        mask_tile = keep.tile([P, PACK - 1, TURNED], F32, name="mask_tile")
-        straddle = twice[:, PLAIN - TURNED // 2 : PLAIN + TURNED // 2]
-        mask = [mask_tile[:, 0, :], mask_tile[:, 1, :], straddle, mask_tile[:, 2, :]]
+        straddle = twice[:, PLAIN - LEAD // 2 : PLAIN + LEAD // 2]
+        mask_last = keep.tile([P, PACK * P], F32, name="mask_last")
+        mask_ends = keep.tile([P, 2, LEAD], F32, name="mask_ends")
+        mask = [mask_ends[:, 0, :], mask_last[:, 0:LEAD], straddle, mask_ends[:, 1, :]]
 
         nc.vector.memset(dy_s[:].bitcast(I32), 0)
         nc.vector.memset(w2_s[:].bitcast(I32), 0)
@@ -77,15 +79,15 @@ def tile_moe_sub_relu2_kernel(
         nc.vector.memset(gate_rows[:], 0.0)
         make_identity(nc, ident[:])
 
+        w2_dst = w2_w[:].rearrange("p (e c) -> p e c", e=E).bitcast(I32)
+        w2_src = w2t_words[:, 0].rearrange("e p c -> p e c").bitcast(I32)
+        nc.sync.dma_start(w2_dst[:, 0:2, :], w2_src[:, 0:2, :])
         nc.sync.dma_start(offs_sb[:], offs)
         dy_rows = dy_scales[0].rearrange("(q r) t -> r q t", r=4)
         for r in range(4):
             queue = nc.scalar if r % 2 else nc.sync
             queue.dma_start(dy_s[r:P:32, :].bitcast(I32), dy_rows[r].bitcast(I32))
-        nc.sync.dma_start(
-            w2_w[:].rearrange("p (e c) -> p e c", e=E).bitcast(I32),
-            w2t_words[:, 0].rearrange("e p c -> p e c").bitcast(I32),
-        )
+        nc.sync.dma_start(w2_dst[:, 2:E, :], w2_src[:, 2:E, :])
         a_rows = a.rearrange("(p d) t -> p d t", d=PACK)
         nc.sync.dma_start(a_turned[:], a_rows[:, :, 0:TURNED])
         nc.sync.dma_start(dy_w[:], dy_words[0].rearrange("p t d -> p (t d)").bitcast(I32))
@@ -108,11 +110,12 @@ def tile_moe_sub_relu2_kernel(
         for r in range(4):
             nc.sync.dma_start(w1_s[r:P:32, :].bitcast(I32), w1_rows[r].bitcast(I32))
 
-        def regroup(d0, words, scales):
-            nc.vector.tensor_copy(
-                words[:].bitcast(U16),
-                w2_w[:].bitcast(U16).rearrange("p (m d) -> p d m", d=PACK)[:, d0 : d0 + 2, :],
-            )
+        def regroup(d0, words, scales, expert_runs):
+            by_plane = w2_w[:].bitcast(U16).rearrange("p (m d) -> p d m", d=PACK)
+            for e0, e1 in expert_runs:
+                nc.vector.tensor_copy(
+                    words[:].bitcast(U16)[:, :, P * e0 : P * e1], by_plane[:, d0 : d0 + 2, P * e0 : P * e1]
+                )
             nc.vector.tensor_copy(scales[:], w2_s[:].rearrange("p (m d) -> p d m", d=PACK)[:, d0 : d0 + 2, :])
 
         def gather_expert(e):
@@ -133,9 +136,8 @@ def tile_moe_sub_relu2_kernel(
             )
             nc.scalar.copy(y[d][:, e * C : (e + 1) * C], acc[:])
 
-        nc.scalar.activation(mask_tile[:, 0:2, :], a_turned[:, 0:2, :], RELU)
-        for d in range(2, PACK):
-            nc.scalar.activation(mask[d], a_turned[:, d, :], RELU)
+        for d in range(PACK):
+            nc.scalar.activation(mask[d], a_turned[:, d, 0:LEAD], RELU)
         gate_ps = psum.tile([P, P], F32, name="turned", bufs=TURN_BANKS)
         nc.tensor.transpose(gate_ps[:], gate_rows[:], ident[:])
         for r in range(2):
@@ -143,14 +145,14 @@ def tile_moe_sub_relu2_kernel(
 
         early_w = keep.tile([P, 2, 2 * E * P], U8, name="early_w", align_bytes=64)
         early_s = keep.tile([P, 2, E * P], U8, name="early_s", align_bytes=64)
-        regroup(0, early_w, early_s)
+        regroup(0, early_w, early_s, ((0, 2), (2, E)))
         for e in range(E):
             gather_expert(e)
             for d in range(2):
                 expert_plane(e, d, early_w, early_s)
         late_w = reuse.tile([P, 2, 2 * E * P], U8, name="late_w", align_bytes=64, offset=0)
         late_s = reuse.tile([P, 2, E * P], U8, name="late_s", align_bytes=64, offset=4 * E * P)
-        regroup(2, late_w, late_s)
+        regroup(2, late_w, late_s, ((0, E),))
         for d in range(2, PACK):
             for e in range(E):
                 expert_plane(e, d, late_w, late_s)
@@ -170,15 +172,20 @@ def tile_moe_sub_relu2_kernel(
             for d in range(PACK):
                 for r in range(2):
                     masked[d, r] = keep.tile([P, TURNED], F32, name="masked%d%d" % (d, r))
-                    gather(masked[d, r][:], d, r, 0, TURNED, mask[d])
-                    for j in range(TILES - 1):
+                    gather(masked[d, r][:, 0:LEAD], d, r, 0, LEAD, mask[d])
+                    for j in range(2):
                         turn(turned[j][r], masked[d, r], d, j)
+            last_planes = mask_last[:].rearrange("p (d t) -> p d t", d=PACK)
+            nc.scalar.activation(last_planes, a_turned[:, :, LEAD:TURNED], RELU)
+            for r in range(2):
+                for d in range(PACK):
+                    gather(masked[d, r][:, LEAD:TURNED], d, r, LEAD, P, last_planes[:, d, :])
             for r in range(2):
                 nc.scalar.activation(gate2[r], gate_sb[r][:], COPY, scale=2.0)
             for j in range(TILES):
                 parts = [keep.tile([P, H], F32, name="part%d_%d" % (r, j)) for r in range(2)]
                 for r in range(2):
-                    if j == TILES - 1:
+                    if j >= 2:
                         for d in range(PACK):
                             turn(turned[j][r], masked[d, r], d, j)
                     nc.scalar.activation(parts[r][:], turned[j][r][:], COPY, scale=gate_cols[r][:, j : j + 1])
@@ -241,7 +248,7 @@ def tile_moe_sub_relu2_kernel(
 
         turned_road()
         plain_road(MIDDLE, ((0, 2), (2, 4)), own_products(MIDDLE), woven_head[:, 2 * MIDDLE[0] :], nc.scalar.copy)
-        quantize(HALF, LATE[0] - HALF, woven_head[:, 2 * HALF :])
+        quantize(MIDDLE[0], MIDDLE[1], woven_head[:, 2 * MIDDLE[0] :])
         plain_road(LATE, ((0, 4),), own_products(LATE), woven_late[:], nc.scalar.copy)
         quantize(LATE[0], LATE[1], woven_late[:])
         quarter = HALF // 2

from contextlib import ExitStack

import concourse.mybir as mybir
from concourse.masks import make_identity

K, T, E, C, H, N = 256, 1024, 4, 512, 512, 512
FLOPS = 2 * N * H * E * C + 2 * H * K * T

F32 = mybir.dt.float32
BF16 = mybir.dt.bfloat16
I32 = mybir.dt.int32
U32 = mybir.dt.uint32
U16 = mybir.dt.uint16
U8 = mybir.dt.uint8
E4M3X4 = mybir.dt.float8_e4m3fn_x4
E5M2X4 = mybir.dt.float8_e5m2_x4
E2M1X4 = mybir.dt.float4_e2m1fn_x4
MULT = mybir.AluOpType.mult
ADD = mybir.AluOpType.add
MAX = mybir.AluOpType.max
COPY = mybir.ActivationFunctionType.Copy
RELU = mybir.ActivationFunctionType.Relu

P = 128
PACK = 4
HALF = 512
LIST_ROWS = 16
TURNED = 512
TILES = TURNED // P
LEAD = TURNED - P
PLAIN = T - TURNED
MIDDLE, LATE, LAST = (TURNED, 2 * P), (768, P), (896, P)
MATMUL_BANKS = 3
TURN_BANKS = 5


def tile_moe_sub_relu2_kernel(
    tc, dy_words, dy_scales, w2t_words, w2t_scales, w1t_words, w1t_scales, a, gate, offs, pos1, pos2, out
):
    nc = tc.nc
    with ExitStack() as ctx:
        keep = ctx.enter_context(tc.tile_pool(name="keep", bufs=1))
        reuse = ctx.enter_context(tc.tile_pool(name="reuse", bufs=1))
        psum = ctx.enter_context(tc.psum_pool(name="psum", bufs=MATMUL_BANKS))

        offs_sb = keep.tile([P, E * C // LIST_ROWS], U16, name="offs_sb")
        pos_sb = [keep.tile([P, T // LIST_ROWS], U16, name="pos%d_sb" % r) for r in range(2)]
        dy_w = reuse.tile([P, T], I32, name="dy_w", align_bytes=64, offset=0)
        dy_s = keep.tile([P, T], U8, name="dy_s", align_bytes=64)
        w2_w = keep.tile([P, E * 2 * H], U8, name="w2_w", align_bytes=64)
        w2_s = keep.tile([P, E * H], U8, name="w2_s", align_bytes=64)
        w1_w = keep.tile([P, K], I32, name="w1_w", align_bytes=64)
        w1_s = keep.tile([P, K], U8, name="w1_s", align_bytes=64)
        gate_sb = [keep.tile([P, PLAIN], F32, name="gate_sb%d" % r) for r in range(2)]
        gate_rows = keep.tile([P, P], F32, name="gate_rows")
        ident = keep.tile([P, P], F32, name="ident")
        a_turned = keep.tile([P, PACK, TURNED], F32, name="a_turned")
        a_plain = keep.tile([P, PACK, PLAIN], F32, name="a_plain")
        slot_w = [keep.tile([P, C], U32, name="slot_w%d" % e, align_bytes=64) for e in range(E)]
        slot_s = [keep.tile([P, C], U8, name="slot_s%d" % e, align_bytes=64) for e in range(E)]
        y = [keep.tile([P, E * C], F32, name="y%d" % d) for d in range(PACK)]
        da_w = [keep.tile([P, HALF], U32, name="da_w%d" % h, align_bytes=64) for h in range(T // HALF)]
        da_s = [keep.tile([P, HALF], U8, name="da_s%d" % h, align_bytes=64) for h in range(T // HALF)]

        woven_head = keep.tile([P, 2 * LATE[0]], F32, name="woven_head", align_bytes=64)
        woven_late = keep.tile([P, 2 * LATE[1]], F32, name="woven_late", align_bytes=64)
        woven_last = keep.tile([P, 2 * LAST[1]], F32, name="woven_last", align_bytes=64)
        gate_cols = [woven_head[:, 2 * MIDDLE[0] : 2 * MIDDLE[0] + TILES], woven_late[:, 0:TILES]]
        twice = keep.tile([P, 2 * PLAIN], F32, name="twice")
        gate2 = [twice[:, r * PLAIN : (r + 1) * PLAIN] for r in range(2)]
        straddle = twice[:, PLAIN - LEAD // 2 : PLAIN + LEAD // 2]
        mask_last = keep.tile([P, PACK * P], F32, name="mask_last")
        mask_ends = keep.tile([P, 2, LEAD], F32, name="mask_ends")
        mask = [mask_ends[:, 0, :], mask_last[:, 0:LEAD], straddle, mask_ends[:, 1, :]]

        nc.vector.memset(dy_s[:].bitcast(I32), 0)
        nc.vector.memset(w2_s[:].bitcast(I32), 0)
        nc.vector.memset(w1_s[:].bitcast(I32), 0)
        nc.vector.memset(gate_rows[:], 0.0)
        make_identity(nc, ident[:])

        w2_dst = w2_w[:].rearrange("p (e c) -> p e c", e=E).bitcast(I32)
        w2_src = w2t_words[:, 0].rearrange("e p c -> p e c").bitcast(I32)
        nc.sync.dma_start(w2_dst[:, 0:2, :], w2_src[:, 0:2, :])
        nc.sync.dma_start(offs_sb[:], offs)
        dy_rows = dy_scales[0].rearrange("(q r) t -> r q t", r=4)
        for r in range(4):
            queue = nc.scalar if r % 2 else nc.sync
            queue.dma_start(dy_s[r:P:32, :].bitcast(I32), dy_rows[r].bitcast(I32))
        nc.sync.dma_start(w2_dst[:, 2:E, :], w2_src[:, 2:E, :])
        a_rows = a.rearrange("(p d) t -> p d t", d=PACK)
        nc.sync.dma_start(a_turned[:], a_rows[:, :, 0:TURNED])
        nc.sync.dma_start(dy_w[:], dy_words[0].rearrange("p t d -> p (t d)").bitcast(I32))
        w2_rows = w2t_scales[:, 0].rearrange("e (q r) c -> r q e c", r=4)
        w1_rows = w1t_scales[0].rearrange("(q r) k -> r q k", r=4)
        for r in range(4):
            nc.scalar.dma_start(
                w2_s[r:P:32, :].rearrange("p (e c) -> p e c", e=E).bitcast(I32), w2_rows[r].bitcast(I32)
            )
        nc.sync.dma_start(pos_sb[0][:], pos1)
        nc.sync.dma_start(pos_sb[1][:], pos2)
        for r in range(2):
            nc.sync.dma_start(
                gate_rows[TILES * r : TILES * (r + 1), :], gate[r, 0, 0:TURNED].rearrange("(j c) -> j c", c=P)
            )
        for r in range(2):
            nc.sync.dma_start(gate_sb[r][:], gate[r, :, TURNED:T])
        nc.sync.dma_start(a_plain[:], a_rows[:, :, TURNED:T])
        nc.sync.dma_start(w1_w[:], w1t_words[0].rearrange("p k d -> p (k d)").bitcast(I32))
        for r in range(4):
            nc.sync.dma_start(w1_s[r:P:32, :].bitcast(I32), w1_rows[r].bitcast(I32))

        def regroup(d0, words, scales, expert_runs):
            by_plane = w2_w[:].bitcast(U16).rearrange("p (m d) -> p d m", d=PACK)
            for e0, e1 in expert_runs:
                nc.vector.tensor_copy(
                    words[:].bitcast(U16)[:, :, P * e0 : P * e1], by_plane[:, d0 : d0 + 2, P * e0 : P * e1]
                )
            nc.vector.tensor_copy(scales[:], w2_s[:].rearrange("p (m d) -> p d m", d=PACK)[:, d0 : d0 + 2, :])

        def gather_expert(e):
            slots = offs_sb[:, e * (C // LIST_ROWS) : (e + 1) * (C // LIST_ROWS)]
            nc.vector.tensor_copy(slot_w[e][:], dy_w[:].bitcast(U32).indirect(slots))
            nc.vector.tensor_copy(slot_s[e][:], dy_s[:].indirect(slots))

        def expert_plane(e, d, words, scales):
            acc = psum.tile([P, C], F32, name="bank")
            nc.tensor.matmul_mx(
                out=acc[:],
                lhsT=words[:, d % 2, 2 * P * e : 2 * P * (e + 1)].bitcast(E2M1X4),
                lhsT_scale=scales[:, d % 2, P * e : P * (e + 1)],
                rhs=slot_w[e][:].bitcast(E5M2X4),
                rhs_scale=slot_s[e][:],
                start=True,
                stop=True,
            )
            nc.scalar.copy(y[d][:, e * C : (e + 1) * C], acc[:])

        for d in range(PACK):
            nc.scalar.activation(mask[d], a_turned[:, d, 0:LEAD], RELU)
        gate_ps = psum.tile([P, P], F32, name="turned", bufs=TURN_BANKS)
        nc.tensor.transpose(gate_ps[:], gate_rows[:], ident[:])
        for r in range(2):
            nc.scalar.activation(gate_cols[r], gate_ps[:, TILES * r : TILES * (r + 1)], COPY, scale=2.0)

        early_w = keep.tile([P, 2, 2 * E * P], U8, name="early_w", align_bytes=64)
        early_s = keep.tile([P, 2, E * P], U8, name="early_s", align_bytes=64)
        regroup(0, early_w, early_s, ((0, 2), (2, E)))
        for e in range(E):
            gather_expert(e)
            for d in range(2):
                expert_plane(e, d, early_w, early_s)
        late_w = reuse.tile([P, 2, 2 * E * P], U8, name="late_w", align_bytes=64, offset=0)
        late_s = reuse.tile([P, 2, E * P], U8, name="late_s", align_bytes=64, offset=4 * E * P)
        regroup(2, late_w, late_s, ((0, E),))
        for d in range(2, PACK):
            for e in range(E):
                expert_plane(e, d, late_w, late_s)

        def gather(dst, d, r, t0, n, factor):
            picks = pos_sb[r][:, t0 // LIST_ROWS : (t0 + n) // LIST_ROWS]
            nc.vector.tensor_tensor(dst, y[d][:].indirect(picks), factor, MULT)

        def turn(bank, masked, d, j):
            nc.tensor.transpose(bank[:, P * d : P * (d + 1)], masked[:, P * j : P * (j + 1)], ident[:])

        def turned_road():
            turned = [
                [psum.tile([P, H], F32, name="turned", bufs=TURN_BANKS) for r in range(2)] for j in range(TILES)
            ]
            masked = {}
            for d in range(PACK):
                for r in range(2):
                    masked[d, r] = keep.tile([P, TURNED], F32, name="masked%d%d" % (d, r))
                    gather(masked[d, r][:, 0:LEAD], d, r, 0, LEAD, mask[d])
                    for j in range(2):
                        turn(turned[j][r], masked[d, r], d, j)
            last_planes = mask_last[:].rearrange("p (d t) -> p d t", d=PACK)
            nc.scalar.activation(last_planes, a_turned[:, :, LEAD:TURNED], RELU)
            for r in range(2):
                for d in range(PACK):
                    gather(masked[d, r][:, LEAD:TURNED], d, r, LEAD, P, last_planes[:, d, :])
            for r in range(2):
                nc.scalar.activation(gate2[r], gate_sb[r][:], COPY, scale=2.0)
            for j in range(TILES):
                parts = [keep.tile([P, H], F32, name="part%d_%d" % (r, j)) for r in range(2)]
                for r in range(2):
                    if j >= 2:
                        for d in range(PACK):
                            turn(turned[j][r], masked[d, r], d, j)
                    nc.scalar.activation(parts[r][:], turned[j][r][:], COPY, scale=gate_cols[r][:, j : j + 1])
                back = psum.tile([P, PACK, P], F32, name="turned", bufs=TURN_BANKS)
                for d in range(PACK):
                    for r in range(2):
                        nc.tensor.matmul(
                            back[:, d, :],
                            parts[r][:, P * d : P * (d + 1)],
                            ident[:],
                            start=(r == 0),
                            stop=(r == 1),
                            is_transpose=True,
                        )
                dst = woven_head[:, 2 * P * j : 2 * P * (j + 1)].bitcast(BF16)
                nc.scalar.copy(dst.rearrange("p (t d) -> p t d", d=PACK), back[:].rearrange("p d t -> p t d"))

        def plain_road(group, cuts, prods, woven, weaver):
            t0, n = group
            c0 = t0 - TURNED
            da = keep.tile([P, PACK, n], BF16, name="da%d" % t0)
            for d0, d1 in cuts:
                for d in range(d0, d1):
                    for r in range(2):
                        gather(prods[r][:, d, :], d, r, t0, n, gate2[r][:, c0 : c0 + n])
                dh = keep.tile([P, d1 - d0, n], F32, name="dh%d_%d" % (t0, d0))
                nc.vector.tensor_tensor(dh[:], prods[0][:, d0:d1, :], prods[1][:, d0:d1, :], ADD)
                nc.vector.scalar_tensor_tensor(da[:, d0:d1, :], a_plain[:, d0:d1, c0 : c0 + n], 0.0, dh[:], MAX, MULT)
            weaver(
                woven.bitcast(BF16).rearrange("p (c i d) -> p c d i", i=4, d=PACK),
                da[:].rearrange("p d (c i) -> p c d i", i=4),
            )

        def own_products(group):
            return [keep.tile([P, PACK, group[1]], F32, name="prod%d_%d" % (r, group[0]))[:] for r in range(2)]

        def quantize(t0, n, woven):
            h, c0 = divmod(t0, HALF)
            nc.vector.quantize_mx(
                out=da_w[h][:, c0 : c0 + n].bitcast(E5M2X4), scales=da_s[h][:, c0 : c0 + n], in_=woven.bitcast(BF16)
            )

        def project(h, movers, pieces):
            width = HALF // pieces
            for kb in range(K // P):
                acc = psum.tile([P, HALF], F32, name="bank")
                nc.tensor.matmul_mx(
                    out=acc[:],
                    lhsT=w1_w[:, P * kb : P * (kb + 1)].bitcast(E4M3X4),
                    lhsT_scale=w1_s[:, P * kb : P * (kb + 1)],
                    rhs=da_w[h][:].bitcast(E5M2X4),
                    rhs_scale=da_s[h][:],
                    start=True,
                    stop=True,
                )
                for c0 in range(0, HALF, width):
                    res = keep.tile([P, width], F32, name="res%d_%d_%d" % (h, kb, c0))
                    movers[kb](res[:], acc[:, c0 : c0 + width])
                    nc.sync.dma_start(out[P * kb : P * (kb + 1), HALF * h + c0 : HALF * h + c0 + width], res[:])

        turned_road()
        plain_road(MIDDLE, ((0, 2), (2, 4)), own_products(MIDDLE), woven_head[:, 2 * MIDDLE[0] :], nc.scalar.copy)
        quantize(MIDDLE[0], MIDDLE[1], woven_head[:, 2 * MIDDLE[0] :])
        plain_road(LATE, ((0, 4),), own_products(LATE), woven_late[:], nc.scalar.copy)
        quantize(LATE[0], LATE[1], woven_late[:])
        quarter = HALF // 2
        for t0 in (0, quarter):
            quantize(t0, quarter, woven_head[:, 2 * t0 : 2 * (t0 + quarter)])
        project(0, (nc.scalar.copy, nc.scalar.copy), 1)
        borrowed = [
            woven_head[:, HALF * r : HALF * (r + 1)].rearrange("p (d t) -> p d t", d=PACK) for r in range(2)
        ]
        plain_road(LAST, ((0, 3), (3, 4)), borrowed, woven_last[:], nc.vector.tensor_copy)
        quantize(LAST[0], LAST[1], woven_last[:])
        project(1, (nc.scalar.copy, nc.vector.tensor_copy), 2)
